import numpy as np
import ml_dtypes


def mxq(x, axis, fmt="e4m3"):
    dtype, down = {"e4m3": (ml_dtypes.float8_e4m3fn, 7), "e5m2": (ml_dtypes.float8_e5m2, 14)}[fmt]
    v = np.moveaxis(np.asarray(x, np.float32).astype(ml_dtypes.bfloat16).astype(np.float64), axis, -1)
    blocks = v.reshape(v.shape[:-1] + (-1, 32))
    amax = np.abs(blocks).max(-1, keepdims=True)
    byte = np.maximum(np.where(amax > 0, np.frexp(amax)[1] - 1 + 127, 0) - down, 1)
    scale = np.exp2(byte - 127.0)
    codes = (blocks / scale).astype(np.float32).astype(dtype).astype(np.float64)
    return np.moveaxis((codes * scale).reshape(v.shape), -1, axis)


WIDE = False


def mx_kscale(k):
    if not WIDE:
        return np.ones(k)
    levels = np.array([10, -10, 5, -5, 0])
    if k % 512:
        return np.exp2(np.random.permutation(np.resize(levels, k // 32))).repeat(32)
    a = np.empty((k // 512, 16))
    for p in range(k // 512):
        a[p, :8] = np.random.permutation(np.resize(levels, 8))
        for g in range(8):
            far = levels[np.abs(levels - a[p, g]) >= 10]
            a[p, g + 8] = far[np.random.randint(len(far))]
    return np.exp2(a.ravel()).repeat(32)


def f64(x):
    return np.asarray(x).astype(np.float64)


def striped(idx):
    return np.tile(idx.reshape(-1, 16).T, (8, 1)).astype(np.uint16)


def unstriped(offs):
    return offs[:16].T.reshape(-1).astype(np.int64)


K, T, E, C, N = 512, 512, 4, 256, 256


def by_expert(wq, xq):
    return np.concatenate([wq[e].T @ xq[:, e * C:(e + 1) * C] for e in range(E)], axis=1)


def setup_inputs():
    n = np.random.standard_normal
    s = mx_kscale(K)[:, None]
    first = np.random.permutation(np.repeat(np.arange(E), T // E))
    second = (first + 1 + np.random.permutation(np.repeat(np.arange(E - 1), -(-T // (E - 1)))[:T])) % E
    while np.bincount(second, minlength=E).max() != T // E:
        load = np.bincount(second, minlength=E); hi, lo = int(load.argmax()), int(load.argmin())
        t = np.flatnonzero((second == hi) & (first != lo))[0]; second[t] = lo
    slot_token = np.empty(E * C, np.int64); pos = np.empty((2, T), np.int64); fill = np.zeros(E, np.int64)
    place = np.stack([np.random.permutation(C) for _ in range(E)])
    for r, deal in enumerate((first, second)):
        for t in np.random.permutation(T):
            e = deal[t]; j = e * C + place[e, fill[e]]; fill[e] += 1; slot_token[j] = t; pos[r, t] = j
    g = np.random.uniform(0.2, 0.8, T)
    return {
        "xT": (n((K, T)) * s).astype(np.float32),
        "w": (n((E, K, N)) / np.sqrt(K) / s[None]).astype(np.float32),
        "gate": np.stack([np.tile(g, (N, 1)), np.tile(1.0 - g, (N, 1))]).astype(np.float32),
        "offs": striped(slot_token),
        "pos1": striped(pos[0]),
        "pos2": striped(pos[1]),
    }


def reference(xT, w, gate, offs, pos1, pos2):
    idx = unstriped(offs)
    xq = mxq(f64(xT)[:, idx], 0, "e4m3")
    y = by_expert(mxq(f64(w), 1, "e4m3"), xq)
    return f64(gate[0]) * y[:, unstriped(pos1)] + f64(gate[1]) * y[:, unstriped(pos2)]

@@ -1,0 +1,163 @@
+from contextlib import ExitStack
+
+import concourse.mybir as mybir
+
+K, T, E, C, N = 512, 512, 4, 256, 256
+FLOPS = 2 * K * N * E * C
+
+F32 = mybir.dt.float32
+BF16 = mybir.dt.bfloat16
+U32 = mybir.dt.uint32
+U16 = mybir.dt.uint16
+U8 = mybir.dt.uint8
+FP8X4 = mybir.dt.float8_e4m3fn_x4
+MULT = mybir.AluOpType.mult
+ADD = mybir.AluOpType.add
+
+P = 128
+PACK = 4
+M_TILES = N // P
+LIST_COLS = C // 16
+
+
+def tile_routed_moe_kernel(tc, xT, w, gate, offs, pos1, pos2, out):
+    nc = tc.nc
+    with ExitStack() as ctx:
+        lists = ctx.enter_context(tc.tile_pool(name="lists", bufs=1))
+        keep = ctx.enter_context(tc.tile_pool(name="keep", bufs=1))
+        turn = ctx.enter_context(tc.tile_pool(name="turn", bufs=1))
+        psum = ctx.enter_context(tc.psum_pool(name="psum", bufs=1))
+
+        offs_t = lists.tile([P, E * C // 16], U16, name="offs_t")
+        nc.sync.dma_start(offs_t[:], offs)
+
+        x_view = xT.rearrange("(p t) n -> p t n", t=PACK)
+        planes = []
+        for t in range(PACK):
+            plane = keep.tile([P, T], F32, name="plane%d" % t)
+            nc.sync.dma_start(plane[:], x_view[:, t, :])
+            planes.append(plane)
+
+        w_raw = []
+        for e in range(E):
+            pool_e = turn if e == E - 1 else keep
+            raw = pool_e.tile([P, PACK, N], F32, name="w_raw%d" % e, tag="s1" if e == E - 1 else "w_raw%d" % e, align_bytes=64)
+            nc.sync.dma_start(raw[:], w[e].rearrange("(p j) n -> p j n", j=PACK))
+            w_raw.append(raw)
+
+        pos1_t = lists.tile([P, T // 16], U16, name="pos1_t")
+        nc.sync.dma_start(pos1_t[:], pos1)
+        pos2_t = lists.tile([P, T // 16], U16, name="pos2_t")
+        nc.sync.dma_start(pos2_t[:], pos2)
+
+        gate_t = {}
+        for m in range(M_TILES):
+            for r in range(2):
+                g = keep.tile([P, T], F32, name="gate%d_%d" % (r, m))
+                nc.sync.dma_start(g[:], gate[r, m * P:(m + 1) * P, :])
+                gate_t[(r, m)] = g
+
+        x_codes = keep.tile([P, E * C], U32, name="x_codes", align_bytes=64)
+        x_scales = keep.tile([P, E * C], U8, name="x_scales", align_bytes=64)
+        w_codes = [keep.tile([P, E * P], U32, name="w_codes0", align_bytes=64), None]
+        w_scales = [keep.tile([P, E * P], U8, name="w_scales%d" % m, align_bytes=64) for m in range(M_TILES)]
+        y_sb = [keep.tile([P, E * C], F32, name="y_sb%d" % m) for m in range(M_TILES)]
+        acc = {}
+        for m in range(M_TILES):
+            pair = psum.tile([P, 2 * C], F32, name="acc%d_01" % m)
+            acc[(m, 0)] = pair[:, 0:C]
+            acc[(m, 1)] = pair[:, C:2 * C]
+            acc[(m, "01")] = pair[:]
+        for e in (2, 3):
+            alone = psum.tile([P, C], F32, name="acc0_%d" % e)
+            acc[(0, e)] = alone[:]
+        pair = psum.tile([P, 2 * C], F32, name="acc1_23")
+        acc[(1, 2)] = pair[:, 0:C]
+        acc[(1, 3)] = pair[:, C:2 * C]
+        acc[(1, "23")] = pair[:]
+
+        wg = [keep.tile([P, E, P, PACK], BF16, name="wg%d" % m, align_bytes=64) for m in range(M_TILES)]
+        g4 = [keep.tile([P, PACK, C], F32, name="g4_%d" % e) for e in range(E)]
+        xg3 = keep.tile([P, C, PACK], BF16, name="xg3", align_bytes=64)
+
+        S = nc.scalar.copy
+        V = nc.vector.tensor_copy
+
+        def gather(e, t):
+            nc.vector.tensor_copy(
+                g4[e][:, t, :], planes[t][:].indirect(offs_t[:, e * LIST_COLS:(e + 1) * LIST_COLS])
+            )
+
+        def group_x(e, dst, eng):
+            eng(out=dst, in_=g4[e][:].rearrange("p t c -> p c t"))
+
+        def group_w(e, m, eng):
+            eng(out=wg[m][:, e, :, :], in_=w_raw[e][:, :, m * P:(m + 1) * P].rearrange("p j n -> p n j"))
+
+        def quant_x(e0, n_experts, src):
+            cols = slice(e0 * C, (e0 + n_experts) * C)
+            nc.vector.quantize_mx(
+                out=x_codes[:, cols].bitcast(FP8X4),
+                scales=x_scales[:, cols],
+                in_=src.rearrange("p c t -> p (c t)"),
+            )
+
+        def quant_w(m):
+            nc.vector.quantize_mx(
+                out=w_codes[m][:].bitcast(FP8X4),
+                scales=w_scales[m][:],
+                in_=wg[m][:].rearrange("p e n j -> p (e n j)"),
+            )
+
+        def multiply(e, m):
+            nc.tensor.matmul_mx(
+                out=acc[(m, e)],
+                lhsT=w_codes[m][:, e * P:(e + 1) * P].bitcast(FP8X4),
+                lhsT_scale=w_scales[m][:, e * P:(e + 1) * P],
+                rhs=x_codes[:, e * C:(e + 1) * C].bitcast(FP8X4),
+                rhs_scale=x_scales[:, e * C:(e + 1) * C],
+                start=True,
+                stop=True,
+            )
+
+        def leave_psum(e0, n_experts, m):
+            key = e0 if n_experts == 1 else "%d%d" % (e0, e0 + 1)
+            nc.scalar.copy(out=y_sb[m][:, e0 * C:(e0 + n_experts) * C], in_=acc[(m, key)])
+
+        for e in range(E):
+            for m in range(M_TILES):
+                group_w(e, m, S)
+        xg012 = turn.tile([P, 3 * C, PACK], BF16, name="xg012", tag="s1", align_bytes=64)
+        for t in range(PACK):
+            for e in range(E):
+                gather(e, t)
+        group_x(0, xg012[:, 0:C, :], S)
+        group_x(1, xg012[:, C:2 * C, :], S)
+        group_x(2, xg012[:, 2 * C:3 * C, :], S)
+        group_x(3, xg3[:], V)
+        quant_w(0)
+        quant_x(3, 1, xg3[:])
+        multiply(3, 0)
+        leave_psum(3, 1, 0)
+        quant_x(0, 2, xg012[:, 0:2 * C, :])
+        multiply(0, 0)
+        multiply(1, 0)
+        leave_psum(0, 2, 0)
+        quant_x(2, 1, xg012[:, 2 * C:3 * C, :])
+        multiply(2, 0)
+        leave_psum(2, 1, 0)
+        w_codes[1] = turn.tile([P, E * P], U32, name="w_codes1", tag="s1", align_bytes=64)
+        quant_w(1)
+        for e in range(E):
+            multiply(e, 1)
+            if e % 2 == 1:
+                leave_psum(e - 1, 2, 1)
+
+        for m in range(M_TILES):
+            first = keep.tile([P, T], F32, name="first%d" % m)
+            nc.vector.tensor_tensor(first[:], y_sb[m][:].indirect(pos1_t[:]), gate_t[(0, m)][:], MULT)
+            second = keep.tile([P, T], F32, name="second%d" % m)
+            nc.vector.tensor_tensor(second[:], y_sb[m][:].indirect(pos2_t[:]), gate_t[(1, m)][:], MULT)
+            total = keep.tile([P, T], F32, name="total%d" % m)
+            nc.vector.tensor_tensor(total[:], first[:], second[:], ADD)
+            nc.sync.dma_start(out[m * P:(m + 1) * P, :], total[:])

@@ -32,16 +32,13 @@ def tile_routed_moe_kernel(tc, xT, w, gate, offs, pos1, pos2, out):
         nc.sync.dma_start(offs_t[:], offs)
 
         x_view = xT.rearrange("(p t) n -> p t n", t=PACK)
-        planes = []
+        x_raw = keep.tile([P, PACK, T], F32, name="x_raw")
         for t in range(PACK):
-            plane = keep.tile([P, T], F32, name="plane%d" % t)
-            nc.sync.dma_start(plane[:], x_view[:, t, :])
-            planes.append(plane)
+            nc.sync.dma_start(x_raw[:, t, :], x_view[:, t, :])
 
         w_raw = []
         for e in range(E):
-            pool_e = turn if e == E - 1 else keep
-            raw = pool_e.tile([P, PACK, N], F32, name="w_raw%d" % e, tag="s1" if e == E - 1 else "w_raw%d" % e, align_bytes=64)
+            raw = keep.tile([P, PACK, N], F32, name="w_raw%d" % e)
             nc.sync.dma_start(raw[:], w[e].rearrange("(p j) n -> p j n", j=PACK))
             w_raw.append(raw)
 
@@ -64,42 +61,32 @@ def tile_routed_moe_kernel(tc, xT, w, gate, offs, pos1, pos2, out):
         y_sb = [keep.tile([P, E * C], F32, name="y_sb%d" % m) for m in range(M_TILES)]
         acc = {}
         for m in range(M_TILES):
-            pair = psum.tile([P, 2 * C], F32, name="acc%d_01" % m)
-            acc[(m, 0)] = pair[:, 0:C]
-            acc[(m, 1)] = pair[:, C:2 * C]
-            acc[(m, "01")] = pair[:]
-        for e in (2, 3):
-            alone = psum.tile([P, C], F32, name="acc0_%d" % e)
-            acc[(0, e)] = alone[:]
-        pair = psum.tile([P, 2 * C], F32, name="acc1_23")
-        acc[(1, 2)] = pair[:, 0:C]
-        acc[(1, 3)] = pair[:, C:2 * C]
-        acc[(1, "23")] = pair[:]
+            for h in range(E // 2):
+                acc[(m, h)] = psum.tile([P, 2 * C], F32, name="acc%d_%d" % (m, h))
 
-        wg = [keep.tile([P, E, P, PACK], BF16, name="wg%d" % m, align_bytes=64) for m in range(M_TILES)]
-        g4 = [keep.tile([P, PACK, C], F32, name="g4_%d" % e) for e in range(E)]
-        xg3 = keep.tile([P, C, PACK], BF16, name="xg3", align_bytes=64)
+        wg = [None, None]
+        wg[0] = turn.tile([P, E, P, PACK], BF16, name="wg0", tag="slot", align_bytes=64)
+        wg[1] = keep.tile([P, E, P, PACK], BF16, name="wg1", align_bytes=64)
+        xg01 = keep.tile([P, 2 * C, PACK], BF16, name="xg01", align_bytes=64)
+        xg2 = keep.tile([P, C, PACK], BF16, name="xg2", align_bytes=64)
 
-        S = nc.scalar.copy
-        V = nc.vector.tensor_copy
+        def gather(e, dst):
+            for t in range(PACK):
+                nc.vector.tensor_copy(
+                    dst[:, :, t], x_raw[:, t, :].indirect(offs_t[:, e * LIST_COLS:(e + 1) * LIST_COLS])
+                )
 
-        def gather(e, t):
-            nc.vector.tensor_copy(
-                g4[e][:, t, :], planes[t][:].indirect(offs_t[:, e * LIST_COLS:(e + 1) * LIST_COLS])
+        def group_w(e, m):
+            nc.scalar.copy(
+                out=wg[m][:, e, :, :], in_=w_raw[e][:, :, m * P:(m + 1) * P].rearrange("p j n -> p n j")
             )
-
-        def group_x(e, dst, eng):
-            eng(out=dst, in_=g4[e][:].rearrange("p t c -> p c t"))
-
-        def group_w(e, m, eng):
-            eng(out=wg[m][:, e, :, :], in_=w_raw[e][:, :, m * P:(m + 1) * P].rearrange("p j n -> p n j"))
 
         def quant_x(e0, n_experts, src):
             cols = slice(e0 * C, (e0 + n_experts) * C)
             nc.vector.quantize_mx(
                 out=x_codes[:, cols].bitcast(FP8X4),
                 scales=x_scales[:, cols],
-                in_=src.rearrange("p c t -> p (c t)"),
+                in_=src[:].rearrange("p c t -> p (c t)"),
             )
 
         def quant_w(m):
@@ -111,7 +98,7 @@ def tile_routed_moe_kernel(tc, xT, w, gate, offs, pos1, pos2, out):
 
         def multiply(e, m):
             nc.tensor.matmul_mx(
-                out=acc[(m, e)],
+                out=acc[(m, e // 2)][:, (e % 2) * C:(e % 2 + 1) * C],
                 lhsT=w_codes[m][:, e * P:(e + 1) * P].bitcast(FP8X4),
                 lhsT_scale=w_scales[m][:, e * P:(e + 1) * P],
                 rhs=x_codes[:, e * C:(e + 1) * C].bitcast(FP8X4),
@@ -121,32 +108,30 @@ def tile_routed_moe_kernel(tc, xT, w, gate, offs, pos1, pos2, out):
             )
 
         def leave_psum(e0, n_experts, m):
-            key = e0 if n_experts == 1 else "%d%d" % (e0, e0 + 1)
-            nc.scalar.copy(out=y_sb[m][:, e0 * C:(e0 + n_experts) * C], in_=acc[(m, key)])
+            lo = (e0 % 2) * C
+            nc.scalar.copy(
+                out=y_sb[m][:, e0 * C:(e0 + n_experts) * C], in_=acc[(m, e0 // 2)][:, lo:lo + n_experts * C]
+            )
 
         for e in range(E):
             for m in range(M_TILES):
-                group_w(e, m, S)
-        xg012 = turn.tile([P, 3 * C, PACK], BF16, name="xg012", tag="s1", align_bytes=64)
-        for t in range(PACK):
-            for e in range(E):
-                gather(e, t)
-        group_x(0, xg012[:, 0:C, :], S)
-        group_x(1, xg012[:, C:2 * C, :], S)
-        group_x(2, xg012[:, 2 * C:3 * C, :], S)
-        group_x(3, xg3[:], V)
+                group_w(e, m)
+        gather(0, xg01[:, 0:C, :])
+        gather(1, xg01[:, C:2 * C, :])
+        gather(2, xg2)
+        quant_x(0, 2, xg01)
+        quant_x(2, 1, xg2)
         quant_w(0)
-        quant_x(3, 1, xg3[:])
+        for e in range(3):
+            multiply(e, 0)
+        leave_psum(0, 2, 0)
+        leave_psum(2, 1, 0)
+        xg3 = turn.tile([P, C, PACK], BF16, name="xg3", tag="slot", align_bytes=64)
+        gather(3, xg3)
+        quant_x(3, 1, xg3)
         multiply(3, 0)
         leave_psum(3, 1, 0)
-        quant_x(0, 2, xg012[:, 0:2 * C, :])
-        multiply(0, 0)
-        multiply(1, 0)
-        leave_psum(0, 2, 0)
-        quant_x(2, 1, xg012[:, 2 * C:3 * C, :])
-        multiply(2, 0)
-        leave_psum(2, 1, 0)
-        w_codes[1] = turn.tile([P, E * P], U32, name="w_codes1", tag="s1", align_bytes=64)
+        w_codes[1] = turn.tile([P, E * P], U32, name="w_codes1", tag="slot", align_bytes=64)
         quant_w(1)
         for e in range(E):
             multiply(e, 1)

@@ -20,6 +20,9 @@ M_TILES = N // P
 LIST_COLS = C // 16
 
 
+GATHER_COLS = (22, 22, 20)
+
+
 def tile_routed_moe_kernel(tc, xT, w, gate, offs, pos1, pos2, out):
     nc = tc.nc
     with ExitStack() as ctx:
@@ -32,15 +35,24 @@ def tile_routed_moe_kernel(tc, xT, w, gate, offs, pos1, pos2, out):
         nc.sync.dma_start(offs_t[:], offs)
 
         x_view = xT.rearrange("(p t) n -> p t n", t=PACK)
-        x_raw = keep.tile([P, PACK, T], F32, name="x_raw")
-        for t in range(PACK):
-            nc.sync.dma_start(x_raw[:, t, :], x_view[:, t, :])
+        planes = [keep.tile([P, T], F32, name="plane%d" % t) for t in range(PACK)]
+        w_raw = [keep.tile([P, PACK, N], F32, name="w_raw%d" % e, align_bytes=64) for e in range(E - 1)]
+        w_raw.append(turn.tile([P, PACK, N], F32, name="w_raw3", tag="s1", align_bytes=64))
 
-        w_raw = []
-        for e in range(E):
-            raw = keep.tile([P, PACK, N], F32, name="w_raw%d" % e)
-            nc.sync.dma_start(raw[:], w[e].rearrange("(p j) n -> p j n", j=PACK))
-            w_raw.append(raw)
+        def load_plane(t):
+            nc.sync.dma_start(planes[t][:], x_view[:, t, :])
+
+        def load_w(e):
+            nc.sync.dma_start(w_raw[e][:], w[e].rearrange("(p j) n -> p j n", j=PACK))
+
+        load_plane(0)
+        load_w(0)
+        load_plane(1)
+        load_w(1)
+        load_plane(2)
+        load_w(2)
+        load_w(3)
+        load_plane(3)
 
         pos1_t = lists.tile([P, T // 16], U16, name="pos1_t")
         nc.sync.dma_start(pos1_t[:], pos1)
@@ -61,44 +73,57 @@ def tile_routed_moe_kernel(tc, xT, w, gate, offs, pos1, pos2, out):
         y_sb = [keep.tile([P, E * C], F32, name="y_sb%d" % m) for m in range(M_TILES)]
         acc = {}
         for m in range(M_TILES):
-            for h in range(E // 2):
-                acc[(m, h)] = psum.tile([P, 2 * C], F32, name="acc%d_%d" % (m, h))
+            pair = psum.tile([P, 2 * C], F32, name="acc%d_01" % m)
+            acc[(m, 0)] = pair[:, 0:C]
+            acc[(m, 1)] = pair[:, C:2 * C]
+            acc[(m, "01")] = pair[:]
+        for e in (2, 3):
+            alone = psum.tile([P, C], F32, name="acc0_%d" % e)
+            acc[(0, e)] = alone[:]
+        pair = psum.tile([P, 2 * C], F32, name="acc1_23")
+        acc[(1, 2)] = pair[:, 0:C]
+        acc[(1, 3)] = pair[:, C:2 * C]
+        acc[(1, "23")] = pair[:]
 
-        wg = [None, None]
-        wg[0] = turn.tile([P, E, P, PACK], BF16, name="wg0", tag="slot", align_bytes=64)
-        wg[1] = keep.tile([P, E, P, PACK], BF16, name="wg1", align_bytes=64)
-        xg01 = keep.tile([P, 2 * C, PACK], BF16, name="xg01", align_bytes=64)
-        xg2 = keep.tile([P, C, PACK], BF16, name="xg2", align_bytes=64)
+        wg = keep.tile([P, M_TILES, E, P, PACK], BF16, name="wg", align_bytes=64)
+        g4 = keep.tile([P, PACK, E * C], F32, name="g4")
+        xg3 = keep.tile([P, C, PACK], BF16, name="xg3", align_bytes=64)
 
-        def gather(e, dst):
-            for t in range(PACK):
+        S = nc.scalar.copy
+        V = nc.vector.tensor_copy
+
+        def gather(t):
+            col = 0
+            for n_cols in GATHER_COLS:
                 nc.vector.tensor_copy(
-                    dst[:, :, t], x_raw[:, t, :].indirect(offs_t[:, e * LIST_COLS:(e + 1) * LIST_COLS])
+                    g4[:, t, 16 * col:16 * (col + n_cols)], planes[t][:].indirect(offs_t[:, col:col + n_cols])
                 )
+                col += n_cols
 
-        def group_w(e, m):
-            nc.scalar.copy(
-                out=wg[m][:, e, :, :], in_=w_raw[e][:, :, m * P:(m + 1) * P].rearrange("p j n -> p n j")
-            )
+        def group_x(e, dst, eng):
+            eng(out=dst, in_=g4[:, :, e * C:(e + 1) * C].rearrange("p t c -> p c t"))
+
+        def group_w(e, eng):
+            eng(out=wg[:, :, e, :, :], in_=w_raw[e][:].rearrange("p j (m n) -> p m n j", m=M_TILES))
 
         def quant_x(e0, n_experts, src):
             cols = slice(e0 * C, (e0 + n_experts) * C)
             nc.vector.quantize_mx(
                 out=x_codes[:, cols].bitcast(FP8X4),
                 scales=x_scales[:, cols],
-                in_=src[:].rearrange("p c t -> p (c t)"),
+                in_=src.rearrange("p c t -> p (c t)"),
             )
 
         def quant_w(m):
             nc.vector.quantize_mx(
                 out=w_codes[m][:].bitcast(FP8X4),
                 scales=w_scales[m][:],
-                in_=wg[m][:].rearrange("p e n j -> p (e n j)"),
+                in_=wg[:, m, :, :, :].rearrange("p e n j -> p (e n j)"),
             )
 
         def multiply(e, m):
             nc.tensor.matmul_mx(
-                out=acc[(m, e // 2)][:, (e % 2) * C:(e % 2 + 1) * C],
+                out=acc[(m, e)],
                 lhsT=w_codes[m][:, e * P:(e + 1) * P].bitcast(FP8X4),
                 lhsT_scale=w_scales[m][:, e * P:(e + 1) * P],
                 rhs=x_codes[:, e * C:(e + 1) * C].bitcast(FP8X4),
@@ -108,30 +133,30 @@ def tile_routed_moe_kernel(tc, xT, w, gate, offs, pos1, pos2, out):
             )
 
         def leave_psum(e0, n_experts, m):
-            lo = (e0 % 2) * C
-            nc.scalar.copy(
-                out=y_sb[m][:, e0 * C:(e0 + n_experts) * C], in_=acc[(m, e0 // 2)][:, lo:lo + n_experts * C]
-            )
+            key = e0 if n_experts == 1 else "%d%d" % (e0, e0 + 1)
+            nc.scalar.copy(out=y_sb[m][:, e0 * C:(e0 + n_experts) * C], in_=acc[(m, key)])
 
         for e in range(E):
-            for m in range(M_TILES):
-                group_w(e, m)
-        gather(0, xg01[:, 0:C, :])
-        gather(1, xg01[:, C:2 * C, :])
-        gather(2, xg2)
-        quant_x(0, 2, xg01)
-        quant_x(2, 1, xg2)
+            group_w(e, S)
+        xg012 = turn.tile([P, 3 * C, PACK], BF16, name="xg012", tag="s1", align_bytes=64)
+        for t in range(PACK):
+            gather(t)
+        group_x(0, xg012[:, 0:C, :], S)
+        group_x(1, xg012[:, C:2 * C, :], S)
+        group_x(2, xg012[:, 2 * C:3 * C, :], S)
+        group_x(3, xg3[:], V)
         quant_w(0)
-        for e in range(3):
-            multiply(e, 0)
-        leave_psum(0, 2, 0)
-        leave_psum(2, 1, 0)
-        xg3 = turn.tile([P, C, PACK], BF16, name="xg3", tag="slot", align_bytes=64)
-        gather(3, xg3)
-        quant_x(3, 1, xg3)
+        quant_x(3, 1, xg3[:])
         multiply(3, 0)
         leave_psum(3, 1, 0)
-        w_codes[1] = turn.tile([P, E * P], U32, name="w_codes1", tag="slot", align_bytes=64)
+        quant_x(0, 2, xg012[:, 0:2 * C, :])
+        multiply(0, 0)
+        multiply(1, 0)
+        leave_psum(0, 2, 0)
+        quant_x(2, 1, xg012[:, 2 * C:3 * C, :])
+        multiply(2, 0)
+        leave_psum(2, 1, 0)
+        w_codes[1] = turn.tile([P, E * P], U32, name="w_codes1", tag="s1", align_bytes=64)
         quant_w(1)
         for e in range(E):
             multiply(e, 1)

@@ -20,7 +20,8 @@ M_TILES = N // P
 LIST_COLS = C // 16
 
 
-GATHER_COLS = (22, 22, 20)
+GATHER_COLS = (32, 32)
+PAD = 16
 
 
 def tile_routed_moe_kernel(tc, xT, w, gate, offs, pos1, pos2, out):
@@ -35,12 +36,12 @@ def tile_routed_moe_kernel(tc, xT, w, gate, offs, pos1, pos2, out):
         nc.sync.dma_start(offs_t[:], offs)
 
         x_view = xT.rearrange("(p t) n -> p t n", t=PACK)
-        planes = [keep.tile([P, T], F32, name="plane%d" % t) for t in range(PACK)]
+        planes = [keep.tile([P, T + PAD], F32, name="plane%d" % t) for t in range(PACK)]
         w_raw = [keep.tile([P, PACK, N], F32, name="w_raw%d" % e, align_bytes=64) for e in range(E - 1)]
         w_raw.append(turn.tile([P, PACK, N], F32, name="w_raw3", tag="s1", align_bytes=64))
 
         def load_plane(t):
-            nc.sync.dma_start(planes[t][:], x_view[:, t, :])
+            nc.sync.dma_start(planes[t][:, 0:T], x_view[:, t, :])
 
         def load_w(e):
             nc.sync.dma_start(w_raw[e][:], w[e].rearrange("(p j) n -> p j n", j=PACK))
@@ -101,10 +102,16 @@ def tile_routed_moe_kernel(tc, xT, w, gate, offs, pos1, pos2, out):
                 col += n_cols
 
         def group_x(e, dst, eng):
-            eng(out=dst, in_=g4[:, :, e * C:(e + 1) * C].rearrange("p t c -> p c t"))
+            eng(
+                out=dst.rearrange("p (c i) t -> p c t i", i=PACK),
+                in_=g4[:, :, e * C:(e + 1) * C].rearrange("p t (c i) -> p c t i", i=PACK),
+            )
 
         def group_w(e, eng):
-            eng(out=wg[:, :, e, :, :], in_=w_raw[e][:].rearrange("p j (m n) -> p m n j", m=M_TILES))
+            eng(
+                out=wg[:, :, e, :, :].rearrange("p m (c i) j -> p m c j i", i=PACK),
+                in_=w_raw[e][:].rearrange("p j (m c i) -> p m c j i", m=M_TILES, i=PACK),
+            )
 
         def quant_x(e0, n_experts, src):
             cols = slice(e0 * C, (e0 + n_experts) * C)

@@ -17,10 +17,6 @@ ADD = mybir.AluOpType.add
 P = 128
 PACK = 4
 M_TILES = N // P
-LIST_COLS = C // 16
-
-
-GATHER_COLS = (32, 32)
 PAD = 16
 
 
@@ -38,7 +34,7 @@ def tile_routed_moe_kernel(tc, xT, w, gate, offs, pos1, pos2, out):
         x_view = xT.rearrange("(p t) n -> p t n", t=PACK)
         planes = [keep.tile([P, T + PAD], F32, name="plane%d" % t) for t in range(PACK)]
         w_raw = [keep.tile([P, PACK, N], F32, name="w_raw%d" % e, align_bytes=64) for e in range(E - 1)]
-        w_raw.append(turn.tile([P, PACK, N], F32, name="w_raw3", tag="s1", align_bytes=64))
+        w_raw.append(turn.tile([P, PACK, N], F32, name="w_raw3", tag="sx", align_bytes=64))
 
         def load_plane(t):
             nc.sync.dma_start(planes[t][:, 0:T], x_view[:, t, :])
@@ -47,13 +43,13 @@ def tile_routed_moe_kernel(tc, xT, w, gate, offs, pos1, pos2, out):
             nc.sync.dma_start(w_raw[e][:], w[e].rearrange("(p j) n -> p j n", j=PACK))
 
         load_plane(0)
-        load_w(0)
         load_plane(1)
-        load_w(1)
         load_plane(2)
+        load_w(0)
+        load_plane(3)
+        load_w(1)
         load_w(2)
         load_w(3)
-        load_plane(3)
 
         pos1_t = lists.tile([P, T // 16], U16, name="pos1_t")
         nc.sync.dma_start(pos1_t[:], pos1)
@@ -87,24 +83,19 @@ def tile_routed_moe_kernel(tc, xT, w, gate, offs, pos1, pos2, out):
         acc[(1, "23")] = pair[:]
 
         wg = keep.tile([P, M_TILES, E, P, PACK], BF16, name="wg", align_bytes=64)
-        g4 = keep.tile([P, PACK, E * C], F32, name="g4")
-        xg3 = keep.tile([P, C, PACK], BF16, name="xg3", align_bytes=64)
+        g4 = [keep.tile([P, PACK, 2 * C], F32, name="g4_01"), None]
 
-        S = nc.scalar.copy
-        V = nc.vector.tensor_copy
+        def gather(t, col0, col1):
+            dst = g4[col0 // 32]
+            nc.vector.tensor_copy(
+                dst[:, t, 16 * (col0 % 32):16 * (col0 % 32) + 16 * (col1 - col0)],
+                planes[t][:].indirect(offs_t[:, col0:col1]),
+            )
 
-        def gather(t):
-            col = 0
-            for n_cols in GATHER_COLS:
-                nc.vector.tensor_copy(
-                    g4[:, t, 16 * col:16 * (col + n_cols)], planes[t][:].indirect(offs_t[:, col:col + n_cols])
-                )
-                col += n_cols
-
-        def group_x(e, dst, eng):
-            eng(
+        def group_x(e, dst):
+            nc.scalar.copy(
                 out=dst.rearrange("p (c i) t -> p c t i", i=PACK),
-                in_=g4[:, :, e * C:(e + 1) * C].rearrange("p t (c i) -> p c t i", i=PACK),
+                in_=g4[e // 2][:, :, (e % 2) * C:(e % 2 + 1) * C].rearrange("p t (c i) -> p c t i", i=PACK),
             )
 
         def group_w(e, eng):
@@ -143,27 +134,36 @@ def tile_routed_moe_kernel(tc, xT, w, gate, offs, pos1, pos2, out):
             key = e0 if n_experts == 1 else "%d%d" % (e0, e0 + 1)
             nc.scalar.copy(out=y_sb[m][:, e0 * C:(e0 + n_experts) * C], in_=acc[(m, key)])
 
-        for e in range(E):
-            group_w(e, S)
-        xg012 = turn.tile([P, 3 * C, PACK], BF16, name="xg012", tag="s1", align_bytes=64)
+        S = nc.scalar.copy
+
         for t in range(PACK):
-            gather(t)
-        group_x(0, xg012[:, 0:C, :], S)
-        group_x(1, xg012[:, C:2 * C, :], S)
-        group_x(2, xg012[:, 2 * C:3 * C, :], S)
-        group_x(3, xg3[:], V)
+            gather(t, 0, 32)
+        group_w(0, S)
+        latch = turn.tile([P, 8], F32, name="latch", tag="sg")
+        nc.scalar.copy(out=latch[:], in_=planes[PACK - 1][:, 0:8])
+        g4[1] = turn.tile([P, PACK, 2 * C], F32, name="g4_23", tag="sg")
+        group_w(1, S)
+        for t in range(PACK):
+            gather(t, 32, 48)
+        group_w(2, S)
+        group_w(3, S)
+        for t in range(PACK):
+            gather(t, 48, 64)
+        xg = turn.tile([P, E * C, PACK], BF16, name="xg", tag="sx", align_bytes=64)
+        for e in range(E):
+            group_x(e, xg[:, e * C:(e + 1) * C, :])
         quant_w(0)
-        quant_x(3, 1, xg3[:])
-        multiply(3, 0)
-        leave_psum(3, 1, 0)
-        quant_x(0, 2, xg012[:, 0:2 * C, :])
+        quant_x(0, 2, xg[:, 0:2 * C, :])
         multiply(0, 0)
         multiply(1, 0)
         leave_psum(0, 2, 0)
-        quant_x(2, 1, xg012[:, 2 * C:3 * C, :])
+        quant_x(2, 1, xg[:, 2 * C:3 * C, :])
         multiply(2, 0)
         leave_psum(2, 1, 0)
-        w_codes[1] = turn.tile([P, E * P], U32, name="w_codes1", tag="s1", align_bytes=64)
+        quant_x(3, 1, xg[:, 3 * C:4 * C, :])
+        multiply(3, 0)
+        leave_psum(3, 1, 0)
+        w_codes[1] = turn.tile([P, E * P], U32, name="w_codes1", tag="sx", align_bytes=64)
         quant_w(1)
         for e in range(E):
             multiply(e, 1)

@@ -33,8 +33,12 @@ def tile_routed_moe_kernel(tc, xT, w, gate, offs, pos1, pos2, out):
 
         x_view = xT.rearrange("(p t) n -> p t n", t=PACK)
         planes = [keep.tile([P, T + PAD], F32, name="plane%d" % t) for t in range(PACK)]
-        w_raw = [keep.tile([P, PACK, N], F32, name="w_raw%d" % e, align_bytes=64) for e in range(E - 1)]
-        w_raw.append(turn.tile([P, PACK, N], F32, name="w_raw3", tag="sx", align_bytes=64))
+        w_raw = [
+            keep.tile([P, PACK, N], F32, name="w_raw0", align_bytes=64),
+            turn.tile([P, PACK, N], F32, name="w_raw1", tag="sa", align_bytes=64),
+            keep.tile([P, PACK, N], F32, name="w_raw2", align_bytes=64),
+            turn.tile([P, PACK, N], F32, name="w_raw3", tag="sx", align_bytes=64),
+        ]
 
         def load_plane(t):
             nc.sync.dma_start(planes[t][:, 0:T], x_view[:, t, :])
@@ -59,7 +63,8 @@ def tile_routed_moe_kernel(tc, xT, w, gate, offs, pos1, pos2, out):
         gate_t = {}
         for m in range(M_TILES):
             for r in range(2):
-                g = keep.tile([P, T], F32, name="gate%d_%d" % (r, m))
+                held = turn if (r, m) == (0, 1) else keep
+                g = held.tile([P, T], F32, name="gate%d_%d" % (r, m), tag="gate%d_%d" % (r, m))
                 nc.sync.dma_start(g[:], gate[r, m * P:(m + 1) * P, :])
                 gate_t[(r, m)] = g
 
@@ -69,18 +74,14 @@ def tile_routed_moe_kernel(tc, xT, w, gate, offs, pos1, pos2, out):
         w_scales = [keep.tile([P, E * P], U8, name="w_scales%d" % m, align_bytes=64) for m in range(M_TILES)]
         y_sb = [keep.tile([P, E * C], F32, name="y_sb%d" % m) for m in range(M_TILES)]
         acc = {}
-        for m in range(M_TILES):
-            pair = psum.tile([P, 2 * C], F32, name="acc%d_01" % m)
-            acc[(m, 0)] = pair[:, 0:C]
-            acc[(m, 1)] = pair[:, C:2 * C]
-            acc[(m, "01")] = pair[:]
-        for e in (2, 3):
+        for e0 in (0, 2):
+            pair = psum.tile([P, 2 * C], F32, name="acc1_%d%d" % (e0, e0 + 1))
+            acc[(1, e0)] = pair[:, 0:C]
+            acc[(1, e0 + 1)] = pair[:, C:2 * C]
+            acc[(1, "%d%d" % (e0, e0 + 1))] = pair[:]
+        for e in range(E):
             alone = psum.tile([P, C], F32, name="acc0_%d" % e)
             acc[(0, e)] = alone[:]
-        pair = psum.tile([P, 2 * C], F32, name="acc1_23")
-        acc[(1, 2)] = pair[:, 0:C]
-        acc[(1, 3)] = pair[:, C:2 * C]
-        acc[(1, "23")] = pair[:]
 
         wg = keep.tile([P, M_TILES, E, P, PACK], BF16, name="wg", align_bytes=64)
         g4 = [keep.tile([P, PACK, 2 * C], F32, name="g4_01"), None]
@@ -92,8 +93,8 @@ def tile_routed_moe_kernel(tc, xT, w, gate, offs, pos1, pos2, out):
                 planes[t][:].indirect(offs_t[:, col0:col1]),
             )
 
-        def group_x(e, dst):
-            nc.scalar.copy(
+        def group_x(e, dst, eng):
+            eng(
                 out=dst.rearrange("p (c i) t -> p c t i", i=PACK),
                 in_=g4[e // 2][:, :, (e % 2) * C:(e % 2 + 1) * C].rearrange("p t (c i) -> p c t i", i=PACK),
             )
@@ -144,23 +145,28 @@ def tile_routed_moe_kernel(tc, xT, w, gate, offs, pos1, pos2, out):
         g4[1] = turn.tile([P, PACK, 2 * C], F32, name="g4_23", tag="sg")
         group_w(1, S)
         for t in range(PACK):
-            gather(t, 32, 48)
+            gather(t, 32, 64)
+        xg01 = turn.tile([P, 2 * C, PACK], BF16, name="xg01", tag="sa", align_bytes=64)
+        group_x(0, xg01[:, 0:C, :], S)
+        group_x(1, xg01[:, C:2 * C, :], S)
         group_w(2, S)
         group_w(3, S)
-        for t in range(PACK):
-            gather(t, 48, 64)
-        xg = turn.tile([P, E * C, PACK], BF16, name="xg", tag="sx", align_bytes=64)
-        for e in range(E):
-            group_x(e, xg[:, e * C:(e + 1) * C, :])
+        latch2 = turn.tile([P, 8], F32, name="latch2", tag="sl", align_bytes=64)
+        nc.scalar.copy(out=latch2[:], in_=w_raw[3][:, 0, 0:8])
+        xg3 = turn.tile([P, C, PACK], BF16, name="xg3", tag="sl", align_bytes=64)
+        xg2 = turn.tile([P, C, PACK], BF16, name="xg2", tag="sx", align_bytes=64)
+        group_x(2, xg2[:], S)
+        quant_x(0, 2, xg01[:])
         quant_w(0)
-        quant_x(0, 2, xg[:, 0:2 * C, :])
         multiply(0, 0)
+        leave_psum(0, 1, 0)
         multiply(1, 0)
-        leave_psum(0, 2, 0)
-        quant_x(2, 1, xg[:, 2 * C:3 * C, :])
+        leave_psum(1, 1, 0)
+        group_x(3, xg3[:], nc.vector.tensor_copy)
+        quant_x(2, 1, xg2[:])
         multiply(2, 0)
         leave_psum(2, 1, 0)
-        quant_x(3, 1, xg[:, 3 * C:4 * C, :])
+        quant_x(3, 1, xg3[:])
         multiply(3, 0)
         leave_psum(3, 1, 0)
         w_codes[1] = turn.tile([P, E * P], U32, name="w_codes1", tag="sx", align_bytes=64)
@@ -170,11 +176,20 @@ def tile_routed_moe_kernel(tc, xT, w, gate, offs, pos1, pos2, out):
             if e % 2 == 1:
                 leave_psum(e - 1, 2, 1)
 
-        for m in range(M_TILES):
-            first = keep.tile([P, T], F32, name="first%d" % m)
-            nc.vector.tensor_tensor(first[:], y_sb[m][:].indirect(pos1_t[:]), gate_t[(0, m)][:], MULT)
-            second = keep.tile([P, T], F32, name="second%d" % m)
-            nc.vector.tensor_tensor(second[:], y_sb[m][:].indirect(pos2_t[:]), gate_t[(1, m)][:], MULT)
-            total = keep.tile([P, T], F32, name="total%d" % m)
-            nc.vector.tensor_tensor(total[:], first[:], second[:], ADD)
+        part = {}
+
+        def fetch(r, m):
+            part[(r, m)] = keep.tile([P, T], F32, name="part%d_%d" % (r, m))
+            nc.vector.tensor_tensor(part[(r, m)][:], y_sb[m][:].indirect((pos1_t, pos2_t)[r][:]), gate_t[(r, m)][:], MULT)
+
+        def finish(m):
+            total = turn.tile([P, T], F32, name="total0", tag="gate0_1") if m == 0 else keep.tile([P, T], F32, name="total1")
+            nc.vector.tensor_tensor(total[:], part[(0, m)][:], part[(1, m)][:], ADD)
             nc.sync.dma_start(out[m * P:(m + 1) * P, :], total[:])
+
+        fetch(0, 0)
+        fetch(1, 0)
+        fetch(0, 1)
+        finish(0)
+        fetch(1, 1)
+        finish(1)

@@ -29,7 +29,6 @@ def tile_routed_moe_kernel(tc, xT, w, gate, offs, pos1, pos2, out):
         psum = ctx.enter_context(tc.psum_pool(name="psum", bufs=1))
 
         offs_t = lists.tile([P, E * C // 16], U16, name="offs_t")
-        nc.sync.dma_start(offs_t[:], offs)
 
         x_view = xT.rearrange("(p t) n -> p t n", t=PACK)
         planes = [keep.tile([P, T + PAD], F32, name="plane%d" % t) for t in range(PACK)]
@@ -46,7 +45,8 @@ def tile_routed_moe_kernel(tc, xT, w, gate, offs, pos1, pos2, out):
         def load_w(e):
             nc.sync.dma_start(w_raw[e][:], w[e].rearrange("(p j) n -> p j n", j=PACK))
 
-        load_plane(0)
+        nc.scalar.dma_start(planes[0][:, 0:T], x_view[:, 0, :])
+        nc.sync.dma_start(offs_t[:], offs)
         load_plane(1)
         load_plane(2)
         load_w(0)

@@ -13,6 +13,7 @@ U8 = mybir.dt.uint8
 FP8X4 = mybir.dt.float8_e4m3fn_x4
 MULT = mybir.AluOpType.mult
 ADD = mybir.AluOpType.add
+COPY = mybir.ActivationFunctionType.Copy
 
 P = 128
 PACK = 4
@@ -34,7 +35,7 @@ def tile_routed_moe_kernel(tc, xT, w, gate, offs, pos1, pos2, out):
         planes = [keep.tile([P, T + PAD], F32, name="plane%d" % t) for t in range(PACK)]
         w_raw = [
             keep.tile([P, PACK, N], F32, name="w_raw0", align_bytes=64),
-            turn.tile([P, PACK, N], F32, name="w_raw1", tag="sa", align_bytes=64),
+            keep.tile([P, PACK, N], F32, name="w_raw1", align_bytes=64),
             keep.tile([P, PACK, N], F32, name="w_raw2", align_bytes=64),
             turn.tile([P, PACK, N], F32, name="w_raw3", tag="sx", align_bytes=64),
         ]
@@ -50,8 +51,8 @@ def tile_routed_moe_kernel(tc, xT, w, gate, offs, pos1, pos2, out):
         load_plane(1)
         load_plane(2)
         load_w(0)
-        load_plane(3)
         load_w(1)
+        load_plane(3)
         load_w(2)
         load_w(3)
 
@@ -68,113 +69,110 @@ def tile_routed_moe_kernel(tc, xT, w, gate, offs, pos1, pos2, out):
                 nc.sync.dma_start(g[:], gate[r, m * P:(m + 1) * P, :])
                 gate_t[(r, m)] = g
 
-        x_codes = keep.tile([P, E * C], U32, name="x_codes", align_bytes=64)
+        bf_planes = [keep.tile([P, T], BF16, name="bf_plane%d" % t) for t in range(PACK)]
+        g2 = keep.tile([P, 2, 2 * C], F32, name="g2")
+        xg = [
+            keep.tile([P, 2 * C, PACK], BF16, name="xg01", align_bytes=64),
+            keep.tile([P, 2 * C, PACK], BF16, name="xg23", align_bytes=64),
+        ]
+        wg = keep.tile([P, E, M_TILES, P, PACK], BF16, name="wg", align_bytes=64)
+        w_codes = keep.tile([P, E * M_TILES * P], U32, name="w_codes", align_bytes=64)
+        w_scales = keep.tile([P, E * M_TILES * P], U8, name="w_scales", align_bytes=64)
         x_scales = keep.tile([P, E * C], U8, name="x_scales", align_bytes=64)
-        w_codes = [keep.tile([P, E * P], U32, name="w_codes0", align_bytes=64), None]
-        w_scales = [keep.tile([P, E * P], U8, name="w_scales%d" % m, align_bytes=64) for m in range(M_TILES)]
         y_sb = [keep.tile([P, E * C], F32, name="y_sb%d" % m) for m in range(M_TILES)]
         acc = {}
-        for e0 in (0, 2):
-            pair = psum.tile([P, 2 * C], F32, name="acc1_%d%d" % (e0, e0 + 1))
-            acc[(1, e0)] = pair[:, 0:C]
-            acc[(1, e0 + 1)] = pair[:, C:2 * C]
-            acc[(1, "%d%d" % (e0, e0 + 1))] = pair[:]
-        for e in range(E):
-            alone = psum.tile([P, C], F32, name="acc0_%d" % e)
-            acc[(0, e)] = alone[:]
+        for m in range(M_TILES):
+            for e in range(E):
+                acc[(m, e)] = psum.tile([P, C], F32, name="acc%d_%d" % (m, e))
 
-        wg = keep.tile([P, M_TILES, E, P, PACK], BF16, name="wg", align_bytes=64)
-        g4 = [keep.tile([P, PACK, 2 * C], F32, name="g4_01"), None]
+        def cast(t):
+            nc.vector.tensor_copy(out=bf_planes[t][:], in_=planes[t][:, 0:T])
 
-        def gather(t, col0, col1):
-            dst = g4[col0 // 32]
+        def gather_v(t):
+            nc.vector.tensor_copy(g2[:, t, :], planes[t][:].indirect(offs_t[:, 32:64]))
+
+        def gather_s(t, e):
+            nc.scalar.activation(
+                xg[e // 2][:, (e % 2) * C:(e % 2 + 1) * C, t],
+                bf_planes[t][:].indirect(offs_t[:, 16 * e:16 * (e + 1)]),
+                COPY,
+            )
+
+        def group_x23():
             nc.vector.tensor_copy(
-                dst[:, t, 16 * (col0 % 32):16 * (col0 % 32) + 16 * (col1 - col0)],
-                planes[t][:].indirect(offs_t[:, col0:col1]),
+                out=xg[1][:, :, 0:2].rearrange("p (c i) t -> p c t i", i=PACK),
+                in_=g2[:].rearrange("p t (c i) -> p c t i", i=PACK),
             )
 
-        def group_x(e, dst, eng):
-            eng(
-                out=dst.rearrange("p (c i) t -> p c t i", i=PACK),
-                in_=g4[e // 2][:, :, (e % 2) * C:(e % 2 + 1) * C].rearrange("p t (c i) -> p c t i", i=PACK),
-            )
-
-        def group_w(e, eng):
-            eng(
-                out=wg[:, :, e, :, :].rearrange("p m (c i) j -> p m c j i", i=PACK),
+        def group_w(e):
+            nc.vector.tensor_copy(
+                out=wg[:, e, :, :, :].rearrange("p m (c i) j -> p m c j i", i=PACK),
                 in_=w_raw[e][:].rearrange("p j (m c i) -> p m c j i", m=M_TILES, i=PACK),
             )
 
-        def quant_x(e0, n_experts, src):
-            cols = slice(e0 * C, (e0 + n_experts) * C)
+        def quant_w(e0):
+            cols = slice(e0 * N, (e0 + 2) * N)
+            nc.vector.quantize_mx(
+                out=w_codes[:, cols].bitcast(FP8X4),
+                scales=w_scales[:, cols],
+                in_=wg[:, e0:e0 + 2, :, :, :].rearrange("p e m n j -> p (e m n j)"),
+            )
+
+        def quant_x(e):
+            cols = slice(e * C, (e + 1) * C)
             nc.vector.quantize_mx(
                 out=x_codes[:, cols].bitcast(FP8X4),
                 scales=x_scales[:, cols],
-                in_=src.rearrange("p c t -> p (c t)"),
-            )
-
-        def quant_w(m):
-            nc.vector.quantize_mx(
-                out=w_codes[m][:].bitcast(FP8X4),
-                scales=w_scales[m][:],
-                in_=wg[:, m, :, :, :].rearrange("p e n j -> p (e n j)"),
+                in_=xg[e // 2][:, (e % 2) * C:(e % 2 + 1) * C, :].rearrange("p c t -> p (c t)"),
             )
 
         def multiply(e, m):
+            wcols = slice((e * M_TILES + m) * P, (e * M_TILES + m + 1) * P)
             nc.tensor.matmul_mx(
-                out=acc[(m, e)],
-                lhsT=w_codes[m][:, e * P:(e + 1) * P].bitcast(FP8X4),
-                lhsT_scale=w_scales[m][:, e * P:(e + 1) * P],
+                out=acc[(m, e)][:],
+                lhsT=w_codes[:, wcols].bitcast(FP8X4),
+                lhsT_scale=w_scales[:, wcols],
                 rhs=x_codes[:, e * C:(e + 1) * C].bitcast(FP8X4),
                 rhs_scale=x_scales[:, e * C:(e + 1) * C],
                 start=True,
                 stop=True,
             )
 
-        def leave_psum(e0, n_experts, m):
-            key = e0 if n_experts == 1 else "%d%d" % (e0, e0 + 1)
-            nc.scalar.copy(out=y_sb[m][:, e0 * C:(e0 + n_experts) * C], in_=acc[(m, key)])
+        def leave_psum(e, m, eng):
+            eng(out=y_sb[m][:, e * C:(e + 1) * C], in_=acc[(m, e)][:])
 
         S = nc.scalar.copy
+        V = nc.vector.tensor_copy
 
-        for t in range(PACK):
-            gather(t, 0, 32)
-        group_w(0, S)
-        latch = turn.tile([P, 8], F32, name="latch", tag="sg")
-        nc.scalar.copy(out=latch[:], in_=planes[PACK - 1][:, 0:8])
-        g4[1] = turn.tile([P, PACK, 2 * C], F32, name="g4_23", tag="sg")
-        group_w(1, S)
-        for t in range(PACK):
-            gather(t, 32, 64)
-        xg01 = turn.tile([P, 2 * C, PACK], BF16, name="xg01", tag="sa", align_bytes=64)
-        group_x(0, xg01[:, 0:C, :], S)
-        group_x(1, xg01[:, C:2 * C, :], S)
-        group_w(2, S)
-        group_w(3, S)
-        latch2 = turn.tile([P, 8], F32, name="latch2", tag="sl", align_bytes=64)
-        nc.scalar.copy(out=latch2[:], in_=w_raw[3][:, 0, 0:8])
-        xg3 = turn.tile([P, C, PACK], BF16, name="xg3", tag="sl", align_bytes=64)
-        xg2 = turn.tile([P, C, PACK], BF16, name="xg2", tag="sx", align_bytes=64)
-        group_x(2, xg2[:], S)
-        quant_x(0, 2, xg01[:])
-        quant_w(0)
-        multiply(0, 0)
-        leave_psum(0, 1, 0)
-        multiply(1, 0)
-        leave_psum(1, 1, 0)
-        group_x(3, xg3[:], nc.vector.tensor_copy)
-        quant_x(2, 1, xg2[:])
-        multiply(2, 0)
-        leave_psum(2, 1, 0)
-        quant_x(3, 1, xg3[:])
-        multiply(3, 0)
-        leave_psum(3, 1, 0)
-        w_codes[1] = turn.tile([P, E * P], U32, name="w_codes1", tag="sx", align_bytes=64)
-        quant_w(1)
+        cast(0)
+        gather_s(0, 0)
+        gather_s(0, 1)
+        gather_v(0)
+        cast(1)
+        gather_s(1, 0)
+        gather_s(1, 1)
+        gather_v(1)
+        cast(2)
         for e in range(E):
+            gather_s(2, e)
+        group_x23()
+        group_w(0)
+        group_w(1)
+        cast(3)
+        for e in range(E):
+            gather_s(3, e)
+        quant_w(0)
+        group_w(2)
+        group_w(3)
+        x_codes = turn.tile([P, E * C], U32, name="x_codes", tag="sx", align_bytes=64)
+        quant_w(2)
+        for e in range(E):
+            quant_x(e)
+            multiply(e, 0)
             multiply(e, 1)
-            if e % 2 == 1:
-                leave_psum(e - 1, 2, 1)
+            leave_psum(e, 0, V if e < 2 else S)
+        for e in range(E):
+            leave_psum(e, 1, S)
 
         part = {}
 

@@ -1,6 +1,7 @@
 from contextlib import ExitStack
 
 import concourse.mybir as mybir
+from concourse.masks import make_identity
 
 K, T, E, C, N = 512, 512, 4, 256, 256
 FLOPS = 2 * K * N * E * C
@@ -19,6 +20,7 @@ P = 128
 PACK = 4
 M_TILES = N // P
 PAD = 16
+PE_COLS = 400
 
 
 def tile_routed_moe_kernel(tc, xT, w, gate, offs, pos1, pos2, out):
@@ -28,6 +30,13 @@ def tile_routed_moe_kernel(tc, xT, w, gate, offs, pos1, pos2, out):
         keep = ctx.enter_context(tc.tile_pool(name="keep", bufs=1))
         turn = ctx.enter_context(tc.tile_pool(name="turn", bufs=1))
         psum = ctx.enter_context(tc.psum_pool(name="psum", bufs=1))
+
+        warm = keep.tile([P, 2], F32, name="warm")
+        nc.vector.memset(warm[:, 0:1], 0.0)
+        nc.scalar.activation(warm[:, 1:2], warm[:, 0:1], COPY)
+
+        ident = keep.tile([P, P], F32, name="ident")
+        make_identity(nc, ident[:])
 
         offs_t = lists.tile([P, E * C // 16], U16, name="offs_t")
 
@@ -73,17 +82,23 @@ def tile_routed_moe_kernel(tc, xT, w, gate, offs, pos1, pos2, out):
         g2 = keep.tile([P, 2, 2 * C], F32, name="g2")
         xg = [
             keep.tile([P, 2 * C, PACK], BF16, name="xg01", align_bytes=64),
-            keep.tile([P, 2 * C, PACK], BF16, name="xg23", align_bytes=64),
+            turn.tile([P, 2 * C, PACK], BF16, name="xg23", tag="sq", align_bytes=64),
         ]
-        wg = keep.tile([P, E, M_TILES, P, PACK], BF16, name="wg", align_bytes=64)
-        w_codes = keep.tile([P, E * M_TILES * P], U32, name="w_codes", align_bytes=64)
-        w_scales = keep.tile([P, E * M_TILES * P], U8, name="w_scales", align_bytes=64)
+        wg = keep.tile([P, M_TILES, E, P, PACK], BF16, name="wg", align_bytes=64)
+        w_codes = [keep.tile([P, E * P], U32, name="w_codes0", align_bytes=64), None]
+        w_scales = [keep.tile([P, E * P], U8, name="w_scales%d" % m, align_bytes=64) for m in range(M_TILES)]
         x_scales = keep.tile([P, E * C], U8, name="x_scales", align_bytes=64)
         y_sb = [keep.tile([P, E * C], F32, name="y_sb%d" % m) for m in range(M_TILES)]
         acc = {}
-        for m in range(M_TILES):
-            for e in range(E):
-                acc[(m, e)] = psum.tile([P, C], F32, name="acc%d_%d" % (m, e))
+        for e0 in (0, 2):
+            pair = psum.tile([P, 2 * C], F32, name="acc1_%d%d" % (e0, e0 + 1))
+            acc[(1, e0)] = pair[:, 0:C]
+            acc[(1, e0 + 1)] = pair[:, C:2 * C]
+            acc[(1, "%d%d" % (e0, e0 + 1))] = pair[:]
+        for e in range(E):
+            alone = psum.tile([P, C], F32, name="acc0_%d" % e)
+            acc[(0, e)] = alone[:]
+        sum_ps = psum.tile([P, PE_COLS], F32, name="sum_ps")
 
         def cast(t):
             nc.vector.tensor_copy(out=bf_planes[t][:], in_=planes[t][:, 0:T])
@@ -106,16 +121,15 @@ def tile_routed_moe_kernel(tc, xT, w, gate, offs, pos1, pos2, out):
 
         def group_w(e):
             nc.vector.tensor_copy(
-                out=wg[:, e, :, :, :].rearrange("p m (c i) j -> p m c j i", i=PACK),
+                out=wg[:, :, e, :, :].rearrange("p m (c i) j -> p m c j i", i=PACK),
                 in_=w_raw[e][:].rearrange("p j (m c i) -> p m c j i", m=M_TILES, i=PACK),
             )
 
-        def quant_w(e0):
-            cols = slice(e0 * N, (e0 + 2) * N)
+        def quant_w(m):
             nc.vector.quantize_mx(
-                out=w_codes[:, cols].bitcast(FP8X4),
-                scales=w_scales[:, cols],
-                in_=wg[:, e0:e0 + 2, :, :, :].rearrange("p e m n j -> p (e m n j)"),
+                out=w_codes[m][:].bitcast(FP8X4),
+                scales=w_scales[m][:],
+                in_=wg[:, m, :, :, :].rearrange("p e n j -> p (e n j)"),
             )
 
         def quant_x(e):
@@ -127,19 +141,19 @@ def tile_routed_moe_kernel(tc, xT, w, gate, offs, pos1, pos2, out):
             )
 
         def multiply(e, m):
-            wcols = slice((e * M_TILES + m) * P, (e * M_TILES + m + 1) * P)
             nc.tensor.matmul_mx(
-                out=acc[(m, e)][:],
-                lhsT=w_codes[:, wcols].bitcast(FP8X4),
-                lhsT_scale=w_scales[:, wcols],
+                out=acc[(m, e)],
+                lhsT=w_codes[m][:, e * P:(e + 1) * P].bitcast(FP8X4),
+                lhsT_scale=w_scales[m][:, e * P:(e + 1) * P],
                 rhs=x_codes[:, e * C:(e + 1) * C].bitcast(FP8X4),
                 rhs_scale=x_scales[:, e * C:(e + 1) * C],
                 start=True,
                 stop=True,
             )
 
-        def leave_psum(e, m, eng):
-            eng(out=y_sb[m][:, e * C:(e + 1) * C], in_=acc[(m, e)][:])
+        def leave_psum(e0, n_experts, m, eng):
+            key = e0 if n_experts == 1 else "%d%d" % (e0, e0 + 1)
+            eng(out=y_sb[m][:, e0 * C:(e0 + n_experts) * C], in_=acc[(m, key)])
 
         S = nc.scalar.copy
         V = nc.vector.tensor_copy
@@ -161,18 +175,20 @@ def tile_routed_moe_kernel(tc, xT, w, gate, offs, pos1, pos2, out):
         cast(3)
         for e in range(E):
             gather_s(3, e)
-        quant_w(0)
         group_w(2)
         group_w(3)
         x_codes = turn.tile([P, E * C], U32, name="x_codes", tag="sx", align_bytes=64)
-        quant_w(2)
+        quant_w(0)
         for e in range(E):
             quant_x(e)
             multiply(e, 0)
-            multiply(e, 1)
-            leave_psum(e, 0, V if e < 2 else S)
+            leave_psum(e, 1, 0, V if e < 1 else S)
+        w_codes[1] = turn.tile([P, E * P], U32, name="w_codes1", tag="sq", align_bytes=64)
+        quant_w(1)
         for e in range(E):
-            leave_psum(e, 1, S)
+            multiply(e, 1)
+            if e % 2 == 1:
+                leave_psum(e - 1, 2, 1, S)
 
         part = {}
 
@@ -180,13 +196,21 @@ def tile_routed_moe_kernel(tc, xT, w, gate, offs, pos1, pos2, out):
             part[(r, m)] = keep.tile([P, T], F32, name="part%d_%d" % (r, m))
             nc.vector.tensor_tensor(part[(r, m)][:], y_sb[m][:].indirect((pos1_t, pos2_t)[r][:]), gate_t[(r, m)][:], MULT)
 
+        def add_on_tensor(r):
+            nc.tensor.matmul(sum_ps[:], lhsT=ident[:], rhs=part[(r, 0)][:, 0:PE_COLS], start=(r == 0), stop=(r == 1))
+
         def finish(m):
             total = turn.tile([P, T], F32, name="total0", tag="gate0_1") if m == 0 else keep.tile([P, T], F32, name="total1")
-            nc.vector.tensor_tensor(total[:], part[(0, m)][:], part[(1, m)][:], ADD)
+            c0 = PE_COLS if m == 0 else 0
+            if m == 0:
+                nc.scalar.copy(out=total[:, 0:c0], in_=sum_ps[:])
+            nc.vector.tensor_tensor(total[:, c0:T], part[(0, m)][:, c0:T], part[(1, m)][:, c0:T], ADD)
             nc.sync.dma_start(out[m * P:(m + 1) * P, :], total[:])
 
         fetch(0, 0)
+        add_on_tensor(0)
         fetch(1, 0)
+        add_on_tensor(1)
         fetch(0, 1)
         finish(0)
         fetch(1, 1)

@@ -19,8 +19,10 @@ COPY = mybir.ActivationFunctionType.Copy
 P = 128
 PACK = 4
 M_TILES = N // P
-PAD = 16
-PE_COLS = 400
+V_COL0 = 28
+V_SLOTS = E * C - 16 * V_COL0
+PAD = V_SLOTS - T + 16
+PE_COLS = 320
 
 
 def tile_routed_moe_kernel(tc, xT, w, gate, offs, pos1, pos2, out):
@@ -78,14 +80,13 @@ def tile_routed_moe_kernel(tc, xT, w, gate, offs, pos1, pos2, out):
                 nc.sync.dma_start(g[:], gate[r, m * P:(m + 1) * P, :])
                 gate_t[(r, m)] = g
 
-        bf_planes = [keep.tile([P, T], BF16, name="bf_plane%d" % t) for t in range(PACK)]
-        g2 = keep.tile([P, 2, 2 * C], F32, name="g2")
-        xg = [
-            keep.tile([P, 2 * C, PACK], BF16, name="xg01", align_bytes=64),
-            turn.tile([P, 2 * C, PACK], BF16, name="xg23", tag="sq", align_bytes=64),
-        ]
+        bf_planes = [keep.tile([P, T], BF16, name="bf_plane%d" % t) for t in range(PACK - 1)]
+        bf_planes.append(turn.tile([P, T], BF16, name="bf_plane3", tag="sq", align_bytes=64))
+        g2 = keep.tile([P, 2, V_SLOTS], F32, name="g2")
+        xg = keep.tile([P, E * C, PACK], BF16, name="xg", align_bytes=64)
         wg = keep.tile([P, M_TILES, E, P, PACK], BF16, name="wg", align_bytes=64)
-        w_codes = [keep.tile([P, E * P], U32, name="w_codes0", align_bytes=64), None]
+        w_codes = [keep.tile([P, E * P], U32, name="w_codes0", align_bytes=64)]
+        w_codes1 = [keep.tile([P, 2 * P], U32, name="w_codes1a", align_bytes=64), None]
         w_scales = [keep.tile([P, E * P], U8, name="w_scales%d" % m, align_bytes=64) for m in range(M_TILES)]
         x_scales = keep.tile([P, E * C], U8, name="x_scales", align_bytes=64)
         y_sb = [keep.tile([P, E * C], F32, name="y_sb%d" % m) for m in range(M_TILES)]
@@ -95,27 +96,31 @@ def tile_routed_moe_kernel(tc, xT, w, gate, offs, pos1, pos2, out):
             acc[(1, e0)] = pair[:, 0:C]
             acc[(1, e0 + 1)] = pair[:, C:2 * C]
             acc[(1, "%d%d" % (e0, e0 + 1))] = pair[:]
-        for e in range(E):
+        for e in range(E - 1):
             alone = psum.tile([P, C], F32, name="acc0_%d" % e)
             acc[(0, e)] = alone[:]
+        last = [psum.tile([P, C // 2], F32, name="acc0_3%s" % h) for h in "ab"]
         sum_ps = psum.tile([P, PE_COLS], F32, name="sum_ps")
 
         def cast(t):
             nc.vector.tensor_copy(out=bf_planes[t][:], in_=planes[t][:, 0:T])
 
         def gather_v(t):
-            nc.vector.tensor_copy(g2[:, t, :], planes[t][:].indirect(offs_t[:, 32:64]))
+            nc.vector.tensor_copy(g2[:, t, :], planes[t][:].indirect(offs_t[:, V_COL0:E * C // 16]))
 
-        def gather_s(t, e):
+        def gather_s(t, e, half=None):
+            col0, col1 = 16 * e, 16 * (e + 1) if t >= 2 else min(16 * (e + 1), V_COL0)
+            if half is not None:
+                col0, col1 = col0 + 8 * half, col0 + 8 * (half + 1)
             nc.scalar.activation(
-                xg[e // 2][:, (e % 2) * C:(e % 2 + 1) * C, t],
-                bf_planes[t][:].indirect(offs_t[:, 16 * e:16 * (e + 1)]),
+                xg[:, 16 * col0:16 * col1, t],
+                bf_planes[t][:].indirect(offs_t[:, col0:col1]),
                 COPY,
             )
 
         def group_x23():
             nc.vector.tensor_copy(
-                out=xg[1][:, :, 0:2].rearrange("p (c i) t -> p c t i", i=PACK),
+                out=xg[:, 16 * V_COL0:E * C, 0:2].rearrange("p (c i) t -> p c t i", i=PACK),
                 in_=g2[:].rearrange("p t (c i) -> p c t i", i=PACK),
             )
 
@@ -125,28 +130,35 @@ def tile_routed_moe_kernel(tc, xT, w, gate, offs, pos1, pos2, out):
                 in_=w_raw[e][:].rearrange("p j (m c i) -> p m c j i", m=M_TILES, i=PACK),
             )
 
-        def quant_w(m):
+        def quant_w0():
             nc.vector.quantize_mx(
-                out=w_codes[m][:].bitcast(FP8X4),
-                scales=w_scales[m][:],
-                in_=wg[:, m, :, :, :].rearrange("p e n j -> p (e n j)"),
+                out=w_codes[0][:].bitcast(FP8X4),
+                scales=w_scales[0][:],
+                in_=wg[:, 0, :, :, :].rearrange("p e n j -> p (e n j)"),
             )
 
-        def quant_x(e):
-            cols = slice(e * C, (e + 1) * C)
+        def quant_w1(h):
             nc.vector.quantize_mx(
-                out=x_codes[:, cols].bitcast(FP8X4),
-                scales=x_scales[:, cols],
-                in_=xg[e // 2][:, (e % 2) * C:(e % 2 + 1) * C, :].rearrange("p c t -> p (c t)"),
+                out=w_codes1[h][:].bitcast(FP8X4),
+                scales=w_scales[1][:, 2 * h * P:2 * (h + 1) * P],
+                in_=wg[:, 1, 2 * h:2 * (h + 1), :, :].rearrange("p e n j -> p (e n j)"),
             )
 
-        def multiply(e, m):
+        def quant_x(c0, c1):
+            nc.vector.quantize_mx(
+                out=x_codes[:, c0:c1].bitcast(FP8X4),
+                scales=x_scales[:, c0:c1],
+                in_=xg[:, c0:c1, :].rearrange("p c t -> p (c t)"),
+            )
+
+        def multiply(e, m, dst, c0, c1):
+            codes = w_codes[0][:, e * P:(e + 1) * P] if m == 0 else w_codes1[e // 2][:, (e % 2) * P:(e % 2 + 1) * P]
             nc.tensor.matmul_mx(
-                out=acc[(m, e)],
-                lhsT=w_codes[m][:, e * P:(e + 1) * P].bitcast(FP8X4),
+                out=dst,
+                lhsT=codes.bitcast(FP8X4),
                 lhsT_scale=w_scales[m][:, e * P:(e + 1) * P],
-                rhs=x_codes[:, e * C:(e + 1) * C].bitcast(FP8X4),
-                rhs_scale=x_scales[:, e * C:(e + 1) * C],
+                rhs=x_codes[:, c0:c1].bitcast(FP8X4),
+                rhs_scale=x_scales[:, c0:c1],
                 start=True,
                 stop=True,
             )
@@ -173,45 +185,66 @@ def tile_routed_moe_kernel(tc, xT, w, gate, offs, pos1, pos2, out):
         group_w(0)
         group_w(1)
         cast(3)
-        for e in range(E):
+        for e in range(E - 1):
             gather_s(3, e)
+        gather_s(3, E - 1, 0)
+        gather_s(3, E - 1, 1)
         group_w(2)
         group_w(3)
         x_codes = turn.tile([P, E * C], U32, name="x_codes", tag="sx", align_bytes=64)
-        quant_w(0)
-        for e in range(E):
-            quant_x(e)
-            multiply(e, 0)
+        quant_w0()
+        for e in range(E - 1):
+            quant_x(e * C, (e + 1) * C)
+            multiply(e, 0, acc[(0, e)], e * C, (e + 1) * C)
             leave_psum(e, 1, 0, V if e < 1 else S)
-        w_codes[1] = turn.tile([P, E * P], U32, name="w_codes1", tag="sq", align_bytes=64)
-        quant_w(1)
+            if e == 0:
+                quant_w1(0)
+        for h in range(2):
+            c0 = (E - 1) * C + h * (C // 2)
+            quant_x(c0, c0 + C // 2)
+            multiply(E - 1, 0, last[h][:], c0, c0 + C // 2)
+            S(out=y_sb[0][:, c0:c0 + C // 2], in_=last[h][:])
+        w_codes1[1] = turn.tile([P, 2 * P], U32, name="w_codes1b", tag="sq", align_bytes=64)
+        quant_w1(1)
         for e in range(E):
-            multiply(e, 1)
+            multiply(e, 1, acc[(1, e)], e * C, (e + 1) * C)
             if e % 2 == 1:
                 leave_psum(e - 1, 2, 1, S)
 
         part = {}
 
-        def fetch(r, m):
-            part[(r, m)] = keep.tile([P, T], F32, name="part%d_%d" % (r, m))
-            nc.vector.tensor_tensor(part[(r, m)][:], y_sb[m][:].indirect((pos1_t, pos2_t)[r][:]), gate_t[(r, m)][:], MULT)
+        def fetch(r, m, c0=0, c1=T):
+            if c0 == 0:
+                part[(r, m)] = keep.tile([P, T], F32, name="part%d_%d" % (r, m))
+            nc.vector.tensor_tensor(
+                part[(r, m)][:, c0:c1],
+                y_sb[m][:].indirect((pos1_t, pos2_t)[r][:, c0 // 16:c1 // 16]),
+                gate_t[(r, m)][:, c0:c1],
+                MULT,
+            )
 
         def add_on_tensor(r):
             nc.tensor.matmul(sum_ps[:], lhsT=ident[:], rhs=part[(r, 0)][:, 0:PE_COLS], start=(r == 0), stop=(r == 1))
 
-        def finish(m):
-            total = turn.tile([P, T], F32, name="total0", tag="gate0_1") if m == 0 else keep.tile([P, T], F32, name="total1")
-            c0 = PE_COLS if m == 0 else 0
-            if m == 0:
-                nc.scalar.copy(out=total[:, 0:c0], in_=sum_ps[:])
-            nc.vector.tensor_tensor(total[:, c0:T], part[(0, m)][:, c0:T], part[(1, m)][:, c0:T], ADD)
-            nc.sync.dma_start(out[m * P:(m + 1) * P, :], total[:])
+        def finish0():
+            total = turn.tile([P, T], F32, name="total0", tag="gate0_1")
+            nc.scalar.copy(out=total[:, 0:PE_COLS], in_=sum_ps[:])
+            nc.vector.tensor_tensor(total[:, PE_COLS:T], part[(0, 0)][:, PE_COLS:T], part[(1, 0)][:, PE_COLS:T], ADD)
+            nc.sync.dma_start(out[0:P, :], total[:])
+
+        total1 = keep.tile([P, T], F32, name="total1")
+
+        def finish1(c0, c1):
+            nc.vector.tensor_tensor(total1[:, c0:c1], part[(0, 1)][:, c0:c1], part[(1, 1)][:, c0:c1], ADD)
+            nc.sync.dma_start(out[P:2 * P, c0:c1], total1[:, c0:c1])
 
         fetch(0, 0)
         add_on_tensor(0)
         fetch(1, 0)
         add_on_tensor(1)
         fetch(0, 1)
-        finish(0)
-        fetch(1, 1)
-        finish(1)
+        finish0()
+        fetch(1, 1, 0, T // 2)
+        fetch(1, 1, T // 2, T)
+        finish1(0, T // 2)
+        finish1(T // 2, T)

@@ -19,10 +19,10 @@ COPY = mybir.ActivationFunctionType.Copy
 P = 128
 PACK = 4
 M_TILES = N // P
-V_COL0 = 28
+V_COL0 = 30
 V_SLOTS = E * C - 16 * V_COL0
 PAD = V_SLOTS - T + 16
-PE_COLS = 320
+PE_COLS = 256
 
 
 def tile_routed_moe_kernel(tc, xT, w, gate, offs, pos1, pos2, out):

@@ -57,7 +57,8 @@ def tile_routed_moe_kernel(tc, xT, w, gate, offs, pos1, pos2, out):
         def load_w(e):
             nc.sync.dma_start(w_raw[e][:], w[e].rearrange("(p j) n -> p j n", j=PACK))
 
-        nc.scalar.dma_start(planes[0][:, 0:T], x_view[:, 0, :])
+        nc.scalar.dma_start(planes[0][:, 0:T // 2], x_view[:, 0, 0:T // 2])
+        nc.sync.dma_start(planes[0][:, T // 2:T], x_view[:, 0, T // 2:T])
         nc.sync.dma_start(offs_t[:], offs)
         load_plane(1)
         load_plane(2)
@@ -170,7 +171,8 @@ def tile_routed_moe_kernel(tc, xT, w, gate, offs, pos1, pos2, out):
         S = nc.scalar.copy
         V = nc.vector.tensor_copy
 
-        cast(0)
+        nc.vector.tensor_copy(out=bf_planes[0][:, 0:T // 2], in_=planes[0][:, 0:T // 2])
+        nc.vector.tensor_copy(out=bf_planes[0][:, T // 2:T], in_=planes[0][:, T // 2:T])
         gather_s(0, 0)
         gather_s(0, 1)
         gather_v(0)

from contextlib import ExitStack

import concourse.mybir as mybir
from concourse.masks import make_identity

K, T, E, C, N = 512, 512, 4, 256, 256
FLOPS = 2 * K * N * E * C

F32 = mybir.dt.float32
BF16 = mybir.dt.bfloat16
U32 = mybir.dt.uint32
U16 = mybir.dt.uint16
U8 = mybir.dt.uint8
FP8X4 = mybir.dt.float8_e4m3fn_x4
MULT = mybir.AluOpType.mult
ADD = mybir.AluOpType.add
COPY = mybir.ActivationFunctionType.Copy

P = 128
PACK = 4
M_TILES = N // P
V_COL0 = 30
V_SLOTS = E * C - 16 * V_COL0
PAD = V_SLOTS - T + 16
PE_COLS = 256


def tile_routed_moe_kernel(tc, xT, w, gate, offs, pos1, pos2, out):
    nc = tc.nc
    with ExitStack() as ctx:
        lists = ctx.enter_context(tc.tile_pool(name="lists", bufs=1))
        keep = ctx.enter_context(tc.tile_pool(name="keep", bufs=1))
        turn = ctx.enter_context(tc.tile_pool(name="turn", bufs=1))
        psum = ctx.enter_context(tc.psum_pool(name="psum", bufs=1))

        warm = keep.tile([P, 2], F32, name="warm")
        nc.vector.memset(warm[:, 0:1], 0.0)
        nc.scalar.activation(warm[:, 1:2], warm[:, 0:1], COPY)

        ident = keep.tile([P, P], F32, name="ident")
        make_identity(nc, ident[:])

        offs_t = lists.tile([P, E * C // 16], U16, name="offs_t")

        x_view = xT.rearrange("(p t) n -> p t n", t=PACK)
        planes = [keep.tile([P, T + PAD], F32, name="plane%d" % t) for t in range(PACK)]
        w_raw = [
            keep.tile([P, PACK, N], F32, name="w_raw0", align_bytes=64),
            keep.tile([P, PACK, N], F32, name="w_raw1", align_bytes=64),
            keep.tile([P, PACK, N], F32, name="w_raw2", align_bytes=64),
            turn.tile([P, PACK, N], F32, name="w_raw3", tag="sx", align_bytes=64),
        ]

        def load_plane(t):
            nc.sync.dma_start(planes[t][:, 0:T], x_view[:, t, :])

        def load_w(e):
            nc.sync.dma_start(w_raw[e][:], w[e].rearrange("(p j) n -> p j n", j=PACK))

        nc.scalar.dma_start(planes[0][:, 0:T // 2], x_view[:, 0, 0:T // 2])
        nc.sync.dma_start(planes[0][:, T // 2:T], x_view[:, 0, T // 2:T])
        nc.sync.dma_start(offs_t[:], offs)
        load_plane(1)
        load_plane(2)
        load_w(0)
        load_w(1)
        load_plane(3)
        load_w(2)
        load_w(3)

        pos1_t = lists.tile([P, T // 16], U16, name="pos1_t")
        nc.sync.dma_start(pos1_t[:], pos1)
        pos2_t = lists.tile([P, T // 16], U16, name="pos2_t")
        nc.sync.dma_start(pos2_t[:], pos2)

        gate_t = {}
        for m in range(M_TILES):
            for r in range(2):
                held = turn if (r, m) == (0, 1) else keep
                g = held.tile([P, T], F32, name="gate%d_%d" % (r, m), tag="gate%d_%d" % (r, m))
                nc.sync.dma_start(g[:], gate[r, m * P:(m + 1) * P, :])
                gate_t[(r, m)] = g

        bf_planes = [keep.tile([P, T], BF16, name="bf_plane%d" % t) for t in range(PACK - 1)]
        bf_planes.append(turn.tile([P, T], BF16, name="bf_plane3", tag="sq", align_bytes=64))
        g2 = keep.tile([P, 2, V_SLOTS], F32, name="g2")
        xg = keep.tile([P, E * C, PACK], BF16, name="xg", align_bytes=64)
        wg = keep.tile([P, M_TILES, E, P, PACK], BF16, name="wg", align_bytes=64)
        w_codes = [keep.tile([P, E * P], U32, name="w_codes0", align_bytes=64)]
        w_codes1 = [keep.tile([P, 2 * P], U32, name="w_codes1a", align_bytes=64), None]
        w_scales = [keep.tile([P, E * P], U8, name="w_scales%d" % m, align_bytes=64) for m in range(M_TILES)]
        x_scales = keep.tile([P, E * C], U8, name="x_scales", align_bytes=64)
        y_sb = [keep.tile([P, E * C], F32, name="y_sb%d" % m) for m in range(M_TILES)]
        acc = {}
        for e0 in (0, 2):
            pair = psum.tile([P, 2 * C], F32, name="acc1_%d%d" % (e0, e0 + 1))
            acc[(1, e0)] = pair[:, 0:C]
            acc[(1, e0 + 1)] = pair[:, C:2 * C]
            acc[(1, "%d%d" % (e0, e0 + 1))] = pair[:]
        for e in range(E - 1):
            alone = psum.tile([P, C], F32, name="acc0_%d" % e)
            acc[(0, e)] = alone[:]
        last = [psum.tile([P, C // 2], F32, name="acc0_3%s" % h) for h in "ab"]
        sum_ps = psum.tile([P, PE_COLS], F32, name="sum_ps")

        def cast(t):
            nc.vector.tensor_copy(out=bf_planes[t][:], in_=planes[t][:, 0:T])

        def gather_v(t):
            nc.vector.tensor_copy(g2[:, t, :], planes[t][:].indirect(offs_t[:, V_COL0:E * C // 16]))

        def gather_s(t, e, half=None):
            col0, col1 = 16 * e, 16 * (e + 1) if t >= 2 else min(16 * (e + 1), V_COL0)
            if half is not None:
                col0, col1 = col0 + 8 * half, col0 + 8 * (half + 1)
            nc.scalar.activation(
                xg[:, 16 * col0:16 * col1, t],
                bf_planes[t][:].indirect(offs_t[:, col0:col1]),
                COPY,
            )

        def group_x23():
            nc.vector.tensor_copy(
                out=xg[:, 16 * V_COL0:E * C, 0:2].rearrange("p (c i) t -> p c t i", i=PACK),
                in_=g2[:].rearrange("p t (c i) -> p c t i", i=PACK),
            )

        def group_w(e):
            nc.vector.tensor_copy(
                out=wg[:, :, e, :, :].rearrange("p m (c i) j -> p m c j i", i=PACK),
                in_=w_raw[e][:].rearrange("p j (m c i) -> p m c j i", m=M_TILES, i=PACK),
            )

        def quant_w0():
            nc.vector.quantize_mx(
                out=w_codes[0][:].bitcast(FP8X4),
                scales=w_scales[0][:],
                in_=wg[:, 0, :, :, :].rearrange("p e n j -> p (e n j)"),
            )

        def quant_w1(h):
            nc.vector.quantize_mx(
                out=w_codes1[h][:].bitcast(FP8X4),
                scales=w_scales[1][:, 2 * h * P:2 * (h + 1) * P],
                in_=wg[:, 1, 2 * h:2 * (h + 1), :, :].rearrange("p e n j -> p (e n j)"),
            )

        def quant_x(c0, c1):
            nc.vector.quantize_mx(
                out=x_codes[:, c0:c1].bitcast(FP8X4),
                scales=x_scales[:, c0:c1],
                in_=xg[:, c0:c1, :].rearrange("p c t -> p (c t)"),
            )

        def multiply(e, m, dst, c0, c1):
            codes = w_codes[0][:, e * P:(e + 1) * P] if m == 0 else w_codes1[e // 2][:, (e % 2) * P:(e % 2 + 1) * P]
            nc.tensor.matmul_mx(
                out=dst,
                lhsT=codes.bitcast(FP8X4),
                lhsT_scale=w_scales[m][:, e * P:(e + 1) * P],
                rhs=x_codes[:, c0:c1].bitcast(FP8X4),
                rhs_scale=x_scales[:, c0:c1],
                start=True,
                stop=True,
            )

        def leave_psum(e0, n_experts, m, eng):
            key = e0 if n_experts == 1 else "%d%d" % (e0, e0 + 1)
            eng(out=y_sb[m][:, e0 * C:(e0 + n_experts) * C], in_=acc[(m, key)])

        S = nc.scalar.copy
        V = nc.vector.tensor_copy

        nc.vector.tensor_copy(out=bf_planes[0][:, 0:T // 2], in_=planes[0][:, 0:T // 2])
        nc.vector.tensor_copy(out=bf_planes[0][:, T // 2:T], in_=planes[0][:, T // 2:T])
        gather_s(0, 0)
        gather_s(0, 1)
        gather_v(0)
        cast(1)
        gather_s(1, 0)
        gather_s(1, 1)
        gather_v(1)
        cast(2)
        for e in range(E):
            gather_s(2, e)
        group_x23()
        group_w(0)
        group_w(1)
        cast(3)
        for e in range(E - 1):
            gather_s(3, e)
        gather_s(3, E - 1, 0)
        gather_s(3, E - 1, 1)
        group_w(2)
        group_w(3)
        x_codes = turn.tile([P, E * C], U32, name="x_codes", tag="sx", align_bytes=64)
        quant_w0()
        for e in range(E - 1):
            quant_x(e * C, (e + 1) * C)
            multiply(e, 0, acc[(0, e)], e * C, (e + 1) * C)
            leave_psum(e, 1, 0, V if e < 1 else S)
            if e == 0:
                quant_w1(0)
        for h in range(2):
            c0 = (E - 1) * C + h * (C // 2)
            quant_x(c0, c0 + C // 2)
            multiply(E - 1, 0, last[h][:], c0, c0 + C // 2)
            S(out=y_sb[0][:, c0:c0 + C // 2], in_=last[h][:])
        w_codes1[1] = turn.tile([P, 2 * P], U32, name="w_codes1b", tag="sq", align_bytes=64)
        quant_w1(1)
        for e in range(E):
            multiply(e, 1, acc[(1, e)], e * C, (e + 1) * C)
            if e % 2 == 1:
                leave_psum(e - 1, 2, 1, S)

        part = {}

        def fetch(r, m, c0=0, c1=T):
            if c0 == 0:
                part[(r, m)] = keep.tile([P, T], F32, name="part%d_%d" % (r, m))
            nc.vector.tensor_tensor(
                part[(r, m)][:, c0:c1],
                y_sb[m][:].indirect((pos1_t, pos2_t)[r][:, c0 // 16:c1 // 16]),
                gate_t[(r, m)][:, c0:c1],
                MULT,
            )

        def add_on_tensor(r):
            nc.tensor.matmul(sum_ps[:], lhsT=ident[:], rhs=part[(r, 0)][:, 0:PE_COLS], start=(r == 0), stop=(r == 1))

        def finish0():
            total = turn.tile([P, T], F32, name="total0", tag="gate0_1")
            nc.scalar.copy(out=total[:, 0:PE_COLS], in_=sum_ps[:])
            nc.vector.tensor_tensor(total[:, PE_COLS:T], part[(0, 0)][:, PE_COLS:T], part[(1, 0)][:, PE_COLS:T], ADD)
            nc.sync.dma_start(out[0:P, :], total[:])

        total1 = keep.tile([P, T], F32, name="total1")

        def finish1(c0, c1):
            nc.vector.tensor_tensor(total1[:, c0:c1], part[(0, 1)][:, c0:c1], part[(1, 1)][:, c0:c1], ADD)
            nc.sync.dma_start(out[P:2 * P, c0:c1], total1[:, c0:c1])

        fetch(0, 0)
        add_on_tensor(0)
        fetch(1, 0)
        add_on_tensor(1)
        fetch(0, 1)
        finish0()
        fetch(1, 1, 0, T // 2)
        fetch(1, 1, T // 2, T)
        finish1(0, T // 2)
        finish1(T // 2, T)
